import numpy as np, ml_dtypes
CORES = [2,10,34,50,74,82,98,114,130,138,162,178,202,210,226,242]
N = 16
TK, LAY = 256, 4
def setup_inputs(rng):
    return {"x": rng.standard_normal((N, 128, TK), dtype=np.float32).astype(ml_dtypes.bfloat16), "w": (rng.standard_normal((N, 128, LAY * 256), dtype=np.float32) / 16).astype(ml_dtypes.bfloat16)}
def setup_inputs_big(rng):
    d = setup_inputs(rng)
    for k in ("x",): d[k] = (d[k].astype(np.float32) * 1048576.0).astype(d[k].dtype)
    return d
def setup_inputs_small(rng):
    d = setup_inputs(rng)
    for k in ("x",): d[k] = (d[k].astype(np.float32) * (1 / 1048576.0)).astype(d[k].dtype)
    return d
def setup_inputs_apart(rng):
    d = setup_inputs(rng)
    f = (10.0 ** rng.permutation(np.linspace(-1.5, 1.5, N))).astype(np.float32).reshape(N, 1, 1)
    for k in ("x",): d[k] = (d[k].astype(np.float32) * f).astype(d[k].dtype)
    return d
def reference(x, w):
    X, W = x.astype(np.float64), w.astype(np.float64)
    h = list(X)
    for l in range(LAY):
        h = [np.maximum(W[r][:, 256 * l:256 * l + 128].T @ h[r] + W[r][:, 256 * l + 128:256 * l + 256].T @ h[r ^ (1 << l)], 0.0) for r in range(N)]
    return {"y": np.stack(h).astype(ml_dtypes.bfloat16)}

@@ -1,0 +1,78 @@
+from concourse.mybir import AluOpType
+
+LAY, TK, P = 4, 256, 128
+NCH = 1
+CW = TK // NCH
+
+SCRATCH = {
+    "wb": ("sbuf", [P, LAY * 256], "bfloat16"),
+    "zero": ("sbuf", [P, CW], "float32"),
+}
+for _l in range(LAY + 1):
+    SCRATCH["h%d" % _l] = ("sbuf", [P, TK], "bfloat16")
+for _l in range(LAY):
+    SCRATCH["land%d" % _l] = ("sbuf", [P, TK], "bfloat16")
+    for _c in range(NCH):
+        SCRATCH["ps%d_%d" % (_l, _c)] = ("psum", [P, 512], "float32")
+
+SEMAPHORES = ["sw0", "sw1", "zs", "sent"]
+for _c in range(NCH):
+    SEMAPHORES += ["sx%d" % _c, "st%d" % _c]
+    for _l in range(LAY):
+        SEMAPHORES += ["arr%d_%d" % (_l, _c), "mm%d_%d" % (_l, _c), "vd%d_%d" % (_l, _c)]
+
+
+def rank_program(g, core, T, topo):
+    rank = T.rank_of(core)
+    if rank is None:
+        return
+    S = T.sem
+    blocks = [(c * CW, (c + 1) * CW) for c in range(NCH)]
+    dq = [g.sync, g.scalar]
+
+    for c, (a, b) in enumerate(blocks):
+        dq[c % 2].dma_start(T.h0[:, a:b], T.x[:, a:b]).then_inc(S["sx%d" % c], 16)
+    g.sync.dma_start(T.wb[:, 0:256], T.w[:, 0:256]).then_inc(S.sw0, 16)
+    dq[(NCH - 1) % 2].dma_start(T.wb[:, 256:LAY * 256], T.w[:, 256:LAY * 256]).then_inc(S.sw1, 16)
+    g.vector.memset(T.zero[:], 0.0).then_inc(S.zs, 1)
+    g.vector.wait_ge(S.zs, 1)
+
+    sent = 0
+    for l in range(LAY):
+        peer = T.cores[rank ^ (1 << l)]
+        rid, pid = topo.addr(peer, core)
+        mask = topo.mask(core, peer)
+        neng = bin(mask).count("1")
+        h, hn, land = T["h%d" % l], T["h%d" % (l + 1)], T["land%d" % l]
+        u = T.wb[:, 256 * l:256 * l + P]
+        v = T.wb[:, 256 * l + P:256 * l + 256]
+        ready = (lambda c: (S["sx%d" % c], 16)) if l == 0 else (lambda c: (S["vd%d_%d" % (l - 1, c)], 1))
+
+        for c, (a, b) in enumerate(blocks):
+            g.wait_ge(*ready(c))
+            g.remote_dma(out_ap=land[:, a:b], in_ap=h[:, a:b], remote_sem=S["arr%d_%d" % (l, c)], local_sem=S.sent,
+                         pid=pid, routing_id=rid, dma_engine_mask=mask)
+            sent += neng
+
+        if l <= 1:
+            g.tensor.wait_ge(S.sw0 if l == 0 else S.sw1, 16)
+        for c, (a, b) in enumerate(blocks):
+            g.tensor.wait_ge(*ready(c))
+            g.tensor.matmul(T["ps%d_%d" % (l, c)][:, 0:CW], u, h[:, a:b], start=True, stop=False)
+        for c, (a, b) in enumerate(blocks):
+            g.tensor.wait_ge(S["arr%d_%d" % (l, c)], neng)
+            g.tensor.matmul(T["ps%d_%d" % (l, c)][:, 0:CW], v, land[:, a:b], start=False, stop=True).then_inc(
+                S["mm%d_%d" % (l, c)], 1)
+
+        for c, (a, b) in enumerate(blocks):
+            g.vector.wait_ge(S["mm%d_%d" % (l, c)], 1)
+            g.vector.tensor_tensor(out=hn[:, a:b], in0=T["ps%d_%d" % (l, c)][:, 0:CW], in1=T.zero[:],
+                                   op=AluOpType.max).then_inc(S["vd%d_%d" % (l, c)], 1)
+
+    for c, (a, b) in enumerate(blocks):
+        q = dq[c % 2]
+        q.wait_ge(S["vd%d_%d" % (LAY - 1, c)], 1)
+        q.dma_start(T.y[:, a:b], T["h%d" % LAY][:, a:b]).then_inc(S["st%d" % c], 16)
+    for c in range(NCH):
+        dq[c % 2].wait_ge(S["st%d" % c], 16)
+    g.wait_ge(S.sent, sent)

@@ -1,7 +1,7 @@
 from concourse.mybir import AluOpType
 
 LAY, TK, P = 4, 256, 128
-NCH = 1
+NCH = 2
 CW = TK // NCH
 
 SCRATCH = {

from concourse.mybir import AluOpType

LAY, TK, P = 4, 256, 128
NCH = 2
CW = TK // NCH

SCRATCH = {
    "wb": ("sbuf", [P, LAY * 256], "bfloat16"),
    "zero": ("sbuf", [P, CW], "float32"),
}
for _l in range(LAY + 1):
    SCRATCH["h%d" % _l] = ("sbuf", [P, TK], "bfloat16")
for _l in range(LAY):
    SCRATCH["land%d" % _l] = ("sbuf", [P, TK], "bfloat16")
    for _c in range(NCH):
        SCRATCH["ps%d_%d" % (_l, _c)] = ("psum", [P, 512], "float32")

SEMAPHORES = ["sw0", "sw1", "zs", "sent"]
for _c in range(NCH):
    SEMAPHORES += ["sx%d" % _c, "st%d" % _c]
    for _l in range(LAY):
        SEMAPHORES += ["arr%d_%d" % (_l, _c), "mm%d_%d" % (_l, _c), "vd%d_%d" % (_l, _c)]


def rank_program(g, core, T, topo):
    rank = T.rank_of(core)
    if rank is None:
        return
    S = T.sem
    blocks = [(c * CW, (c + 1) * CW) for c in range(NCH)]
    dq = [g.sync, g.scalar]

    for c, (a, b) in enumerate(blocks):
        dq[c % 2].dma_start(T.h0[:, a:b], T.x[:, a:b]).then_inc(S["sx%d" % c], 16)
    g.sync.dma_start(T.wb[:, 0:256], T.w[:, 0:256]).then_inc(S.sw0, 16)
    dq[(NCH - 1) % 2].dma_start(T.wb[:, 256:LAY * 256], T.w[:, 256:LAY * 256]).then_inc(S.sw1, 16)
    g.vector.memset(T.zero[:], 0.0).then_inc(S.zs, 1)
    g.vector.wait_ge(S.zs, 1)

    sent = 0
    for l in range(LAY):
        peer = T.cores[rank ^ (1 << l)]
        rid, pid = topo.addr(peer, core)
        mask = topo.mask(core, peer)
        neng = bin(mask).count("1")
        h, hn, land = T["h%d" % l], T["h%d" % (l + 1)], T["land%d" % l]
        u = T.wb[:, 256 * l:256 * l + P]
        v = T.wb[:, 256 * l + P:256 * l + 256]
        ready = (lambda c: (S["sx%d" % c], 16)) if l == 0 else (lambda c: (S["vd%d_%d" % (l - 1, c)], 1))

        for c, (a, b) in enumerate(blocks):
            g.wait_ge(*ready(c))
            g.remote_dma(out_ap=land[:, a:b], in_ap=h[:, a:b], remote_sem=S["arr%d_%d" % (l, c)], local_sem=S.sent,
                         pid=pid, routing_id=rid, dma_engine_mask=mask)
            sent += neng

        if l <= 1:
            g.tensor.wait_ge(S.sw0 if l == 0 else S.sw1, 16)
        for c, (a, b) in enumerate(blocks):
            g.tensor.wait_ge(*ready(c))
            g.tensor.matmul(T["ps%d_%d" % (l, c)][:, 0:CW], u, h[:, a:b], start=True, stop=False)
        for c, (a, b) in enumerate(blocks):
            g.tensor.wait_ge(S["arr%d_%d" % (l, c)], neng)
            g.tensor.matmul(T["ps%d_%d" % (l, c)][:, 0:CW], v, land[:, a:b], start=False, stop=True).then_inc(
                S["mm%d_%d" % (l, c)], 1)

        for c, (a, b) in enumerate(blocks):
            g.vector.wait_ge(S["mm%d_%d" % (l, c)], 1)
            g.vector.tensor_tensor(out=hn[:, a:b], in0=T["ps%d_%d" % (l, c)][:, 0:CW], in1=T.zero[:],
                                   op=AluOpType.max).then_inc(S["vd%d_%d" % (l, c)], 1)

    for c, (a, b) in enumerate(blocks):
        q = dq[c % 2]
        q.wait_ge(S["vd%d_%d" % (LAY - 1, c)], 1)
        q.dma_start(T.y[:, a:b], T["h%d" % LAY][:, a:b]).then_inc(S["st%d" % c], 16)
    for c in range(NCH):
        dq[c % 2].wait_ge(S["st%d" % c], 16)
    g.wait_ge(S.sent, sent)
